import numpy as np
import ml_dtypes


def mxq(x, axis, fmt="e4m3"):
    dtype, down = {"e4m3": (ml_dtypes.float8_e4m3fn, 7), "e5m2": (ml_dtypes.float8_e5m2, 14)}[fmt]
    v = np.moveaxis(np.asarray(x, np.float32).astype(ml_dtypes.bfloat16).astype(np.float64), axis, -1)
    blocks = v.reshape(v.shape[:-1] + (-1, 32))
    amax = np.abs(blocks).max(-1, keepdims=True)
    byte = np.maximum(np.where(amax > 0, np.frexp(amax)[1] - 1 + 127, 0) - down, 1)
    scale = np.exp2(byte - 127.0)
    codes = (blocks / scale).astype(np.float32).astype(dtype).astype(np.float64)
    return np.moveaxis((codes * scale).reshape(v.shape), -1, axis)


WIDE = False


def mx_kscale(k):
    if not WIDE:
        return np.ones(k)
    levels = np.array([10, -10, 5, -5, 0])
    if k % 512:
        return np.exp2(np.random.permutation(np.resize(levels, k // 32))).repeat(32)
    a = np.empty((k // 512, 16))
    for p in range(k // 512):
        a[p, :8] = np.random.permutation(np.resize(levels, 8))
        for g in range(8):
            far = levels[np.abs(levels - a[p, g]) >= 10]
            a[p, g + 8] = far[np.random.randint(len(far))]
    return np.exp2(a.ravel()).repeat(32)


def f64(x):
    return np.asarray(x).astype(np.float64)


def striped(idx):
    return np.tile(idx.reshape(-1, 16).T, (8, 1)).astype(np.uint16)


def unstriped(offs):
    return offs[:16].T.reshape(-1).astype(np.int64)


def striped8(idx):
    return np.concatenate([x.reshape(-1, 16).T for x in idx]).astype(np.uint16)


def runs(offs, k):
    lists = np.stack([offs[16 * r : 16 * r + 16].T.reshape(-1) for r in range(8)]).astype(np.int64)
    return lists[np.arange(k) % 512 // 64]


def pack_weight(w):
    k, n = w.shape
    w = f64(np.asarray(w, np.float32).astype(ml_dtypes.bfloat16)).reshape(k // 32, 32, n)
    amax = np.abs(w).max(1)
    byte = np.clip(np.where(amax > 0, np.frexp(amax)[1] - 1 + 127 - 7, 1), 1, 254)
    scaled = (w * np.exp2(127.0 - byte)[:, None, :]).reshape(k, n).astype(np.float32)
    words = np.ascontiguousarray(scaled.reshape(k // 512, 128, 4, n).transpose(0, 1, 3, 2)).astype(ml_dtypes.float8_e4m3fn).view(np.uint8)
    return words, np.ascontiguousarray(byte.astype(np.uint8).reshape(k // 512, 16, n))


def unpack_weight(words, scales):
    g, p, n, _ = words.shape
    vals = np.ascontiguousarray(words).view(ml_dtypes.float8_e4m3fn).astype(np.float64) * np.repeat(np.exp2(scales.astype(np.float64) - 127.0), 8, axis=1)[..., None]
    return vals.transpose(0, 1, 3, 2).reshape(g * 512, n)


K, T, S, H, G = 512, 1024, 256, 512, 2048


def setup_inputs():
    n = np.random.standard_normal
    s = mx_kscale(K)[:, None]
    packed_xT = pack_weight(n((K, T)) * s)
    packed_dT = pack_weight(n((K, G)) / s)
    return {
        "x_words": packed_xT[0],
        "x_scales": packed_xT[1],
        "w1": (n((K, H)) / np.sqrt(K) / s).astype(np.float32),
        "gs": (np.random.uniform(0.5, 1.5, (K, 1)) * s).astype(np.float32),
        "d_words": packed_dT[0],
        "d_scales": packed_dT[1],
        "offs": striped(np.random.permutation(T)[:S]),
        "k1": striped8(np.random.randint(0, G, (8, H))),
        "k2": striped8(np.random.randint(0, G, (8, H))),
        "hz": striped8(np.random.randint(0, T, (8, S))),
        "n1": striped(np.random.permutation(S)),
        "n2": striped(np.random.permutation(S)),
    }


def reference(x_words, x_scales, w1, gs, d_words, d_scales, offs, k1, k2, hz, n1, n2):
    d_k1 = unpack_weight(d_words, d_scales)[np.arange(K)[:, None], runs(k1, K)]
    xq = unpack_weight(x_words, x_scales)[:, unstriped(offs)]
    y = mxq(f64(w1), 0, "e4m3").T @ xq
    z = f64(gs) * y
    d_k2 = unpack_weight(d_words, d_scales)[np.arange(K)[:, None], runs(k2, K)]
    x_hz = unpack_weight(x_words, x_scales)[np.arange(K)[:, None], runs(hz, K)]
    h = 0.0625 * ((d_k1.T @ mxq(z, 0, "e4m3") + d_k2.T @ x_hz))
    ds = np.zeros((H, S))
    ds[:, unstriped(n1)] = h
    ds2 = np.zeros((H, S))
    ds2[:, unstriped(n2)] = h
    return np.maximum(ds, ds2)

@@ -1,0 +1,212 @@
+from contextlib import ExitStack
+
+import concourse.mybir as mybir
+
+K, T, S, H, G = 512, 1024, 256, 512, 2048
+FLOPS = 3 * 2 * K * H * S
+
+F32 = mybir.dt.float32
+BF16 = mybir.dt.bfloat16
+I32 = mybir.dt.int32
+U32 = mybir.dt.uint32
+U16 = mybir.dt.uint16
+U8 = mybir.dt.uint8
+FP8X4 = mybir.dt.float8_e4m3fn_x4
+COPY = mybir.ActivationFunctionType.Copy
+MULT = mybir.AluOpType.mult
+MAX = mybir.AluOpType.max
+
+P = 128
+PACK = 4
+HALF_S = S // 2
+HALF_H = H // 2
+WINDOW = 384
+
+
+def entries(lst, first, count):
+    return lst[:, first // 16 : (first + count) // 16]
+
+
+def tile_picked_cmixhisendtwo_none_p_kernel(
+    tc, x_words, x_scales, w1, gs, d_words, d_scales, offs, k1, k2, hz, n1, n2, out
+):
+    nc = tc.nc
+    with ExitStack() as ctx:
+        lists = ctx.enter_context(tc.tile_pool(name="lists", bufs=1))
+        sb = ctx.enter_context(tc.tile_pool(name="sb", bufs=1))
+        psum = ctx.enter_context(tc.psum_pool(name="psum", bufs=1))
+
+        def tile(shape, dtype, name, tag=None):
+            return sb.tile(shape, dtype, name=name, tag=tag or name, align_bytes=64)
+
+        def load_list(src, name):
+            lst = lists.tile([P, src.shape[1]], U16, name=name)
+            nc.sync.dma_start(lst[:], src)
+            return lst
+
+        x_bytes = tile([P, T], U8, "x_bytes")
+        d_bytes = tile([P, G], U8, "d_bytes")
+        nc.vector.memset(x_bytes[:].bitcast(I32), 0)
+        nc.gpsimd.memset(d_bytes[:].bitcast(I32), 0)
+
+        offs_l = load_list(offs, "offs_l")
+        hz_l = load_list(hz, "hz_l")
+        nc.scalar.dma_start(x_bytes[0:P:8, :].bitcast(I32), x_scales[0].bitcast(I32))
+        nc.scalar.dma_start(d_bytes[0:P:8, :].bitcast(I32), d_scales[0].bitcast(I32))
+        k1_l = load_list(k1, "k1_l")
+        k2_l = load_list(k2, "k2_l")
+        w_raw = tile([P, PACK, H], F32, "w_raw")
+        nc.sync.dma_start(w_raw[:], w1.rearrange("(p j) c -> p j c", j=PACK))
+        gains = tile([P, PACK], F32, "gains")
+        nc.sync.dma_start(gains[:], gs.rearrange("(p t) o -> p (t o)", t=PACK))
+        n1_l = load_list(n1, "n1_l")
+        n2_l = load_list(n2, "n2_l")
+        x_table = tile([P, T], I32, "x_table")
+        nc.sync.dma_start(x_table[:], x_words[0].rearrange("p c r -> p (c r)").bitcast(I32))
+        d_table = tile([P, G], I32, "d_table")
+        nc.sync.dma_start(d_table[:], d_words[0].rearrange("p c r -> p (c r)").bitcast(I32))
+
+        def pick_scales(name, tag, picks):
+            picked = tile([P, sum(pick[3] for pick in picks)], U8, name, tag)
+            at = 0
+            for table, lst, first, count in picks:
+                nc.vector.tensor_copy(picked[:, at : at + count], table[:].indirect(entries(lst, first, count)))
+                at = at + count
+            return picked
+
+        def move_scales(name, tag, queue, picked):
+            plane = tile(picked.shape, U8, name, tag)
+            nc.vector.memset(plane[:].bitcast(I32), 0)
+            for b in range(4):
+                queue.dma_start(plane[b:P:32, :].bitcast(I32), picked[8 * b : P : 32, :].bitcast(I32))
+            return plane
+
+        def gather_words(words, table, lst, first, count):
+            nc.vector.tensor_copy(words, table[:].bitcast(U32).indirect(entries(lst, first, count)))
+
+        picked0 = pick_scales(
+            "picked0",
+            None,
+            [(x_bytes, offs_l, 0, S), (x_bytes, hz_l, 0, S), (d_bytes, k1_l, 0, HALF_H), (d_bytes, k2_l, 0, HALF_H)],
+        )
+
+        w_bf = tile([P, PACK, P, PACK], BF16, "w_bf")
+        w_out = w_bf[:].rearrange("p t m j -> p m j t")
+        w_in = w_raw[:].rearrange("p j (m t) -> p m j t", t=PACK)
+        nc.scalar.activation(w_out[:, 48:], w_in[:, 48:], COPY)
+        nc.vector.tensor_copy(w_out[:, :48], w_in[:, :48])
+        plane0 = move_scales("plane0", "w_raw", nc.scalar, picked0)
+        offs_scales, hz_scales = plane0[:, :S], plane0[:, S : 2 * S]
+        k1_scales0, k2_scales0 = plane0[:, 2 * S : 2 * S + HALF_H], plane0[:, 2 * S + HALF_H :]
+
+        x_offs0 = tile([P, HALF_S], U32, "x_offs0")
+        x_hz0 = tile([P, HALF_S], U32, "x_hz0")
+        gather_words(x_offs0[:], x_table, offs_l, 0, HALF_S)
+        gather_words(x_hz0[:], x_table, hz_l, 0, HALF_S)
+        w_codes = tile([P, H], U32, "w_codes")
+        w_scales = tile([P, H], U8, "w_scales")
+        nc.vector.quantize_mx(
+            out=w_codes[:].bitcast(FP8X4), scales=w_scales[:], in_=w_bf[:].rearrange("p t m j -> p (t m j)")
+        )
+
+        def make_z(a, x_offs):
+            y = psum.tile([P, PACK, HALF_S], F32, name=f"y{a}")
+            for t in range(PACK):
+                cols = slice(t * P, (t + 1) * P)
+                nc.tensor.matmul_mx(
+                    out=y[:, t, :],
+                    lhsT=w_codes[:, cols].bitcast(FP8X4),
+                    lhsT_scale=w_scales[:, cols],
+                    rhs=x_offs.bitcast(FP8X4),
+                    rhs_scale=offs_scales[:, a * HALF_S : (a + 1) * HALF_S],
+                    start=True,
+                    stop=True,
+                )
+            z_bf = tile([P, HALF_S, PACK], BF16, f"z_bf{a}")
+            nc.vector.tensor_tensor(
+                z_bf[:],
+                y[:].rearrange("p t j -> p j t"),
+                gains[:].unsqueeze(1).to_broadcast([P, HALF_S, PACK]),
+                MULT,
+            )
+            z_codes = tile([P, HALF_S], U32, f"z_codes{a}")
+            z_scales = tile([P, HALF_S], U8, f"z_scales{a}")
+            nc.vector.quantize_mx(
+                out=z_codes[:].bitcast(FP8X4), scales=z_scales[:], in_=z_bf[:].rearrange("p j t -> p (j t)")
+            )
+            return z_codes[:], z_scales[:]
+
+        def gather_d(c):
+            d_k2 = tile([P, HALF_H], U32, f"d_k2_{c}", "d_k2")
+            d_k1 = tile([P, HALF_H], U32, f"d_k1_{c}", "d_k1")
+            gather_words(d_k2[:], d_table, k2_l, c * HALF_H, HALF_H)
+            gather_words(d_k1[:], d_table, k1_l, c * HALF_H, HALF_H)
+            return d_k1, d_k2
+
+        def make_h(acc, r, a, stationary, moving):
+            d_k1, d_k2, k1_scales, k2_scales = stationary
+            z_codes, z_scales, x_hz = moving
+            cols = slice(r % 2 * P, (r % 2 + 1) * P)
+            nc.tensor.matmul_mx(
+                out=acc,
+                lhsT=d_k2[:, cols].bitcast(FP8X4),
+                lhsT_scale=k2_scales[:, cols],
+                rhs=x_hz.bitcast(FP8X4),
+                rhs_scale=hz_scales[:, a * HALF_S : (a + 1) * HALF_S],
+                start=True,
+                stop=False,
+            )
+            nc.tensor.matmul_mx(
+                out=acc,
+                lhsT=d_k1[:, cols].bitcast(FP8X4),
+                lhsT_scale=k1_scales[:, cols],
+                rhs=z_codes.bitcast(FP8X4),
+                rhs_scale=z_scales,
+                start=False,
+                stop=True,
+            )
+
+        windows = [[tile([P, WINDOW], F32, f"ds{u}_{r}") for u in range(2)] for r in range(H // P)]
+
+        def send(acc, r, first, count):
+            h = tile([P, count], F32, f"h{r}_{first}")
+            if (r, first) == (0, 0):
+                nc.scalar.activation(h[:], acc, COPY, scale=0.0625)
+            else:
+                nc.vector.tensor_scalar_mul(h[:], acc, 0.0625)
+            for window, lst in zip(windows[r], (n1_l, n2_l)):
+                nc.scalar.activation(window[:].indirect(entries(lst, first, count)), h[:], COPY)
+
+        def finish(r, tag):
+            best = tile([P, S], F32, f"best{r}", tag)
+            nc.vector.tensor_tensor(best[:], windows[r][0][:, :S], windows[r][1][:, :S], MAX)
+            nc.sync.dma_start(out[r * P : (r + 1) * P, :], best[:])
+
+        moving0 = (*make_z(0, x_offs0[:]), x_hz0[:])
+        stationary0 = (*gather_d(0), k1_scales0, k2_scales0)
+        for r in range(2):
+            acc = psum.tile([P, HALF_S], F32, name=f"h{r}_0")
+            make_h(acc[:], r, 0, stationary0, moving0)
+            send(acc[:], r, 0, HALF_S)
+
+        x_both1 = tile([P, S], U32, "x_both1", "z_bf0")
+        gather_words(x_both1[:, :HALF_S], x_table, offs_l, HALF_S, HALF_S)
+        gather_words(x_both1[:, HALF_S:], x_table, hz_l, HALF_S, HALF_S)
+        moving1 = (*make_z(1, x_both1[:, :HALF_S]), x_both1[:, HALF_S:])
+        for r in range(2):
+            acc = psum.tile([P, HALF_S], F32, name=f"h{r}_1")
+            make_h(acc[:], r, 1, stationary0, moving1)
+            send(acc[:], r, HALF_S, HALF_S)
+
+        picked1 = pick_scales("picked1", "z_bf1", [(d_bytes, k1_l, HALF_H, HALF_H), (d_bytes, k2_l, HALF_H, HALF_H)])
+        plane1 = move_scales("plane1", None, nc.sync, picked1)
+        k1_scales1, k2_scales1 = plane1[:, :HALF_H], plane1[:, HALF_H:]
+        stationary1 = (*gather_d(1), k1_scales1, k2_scales1)
+        for r in range(2, 4):
+            acc = psum.tile([P, S], F32, name=f"h{r}")
+            for a, moving in enumerate((moving0, moving1)):
+                make_h(acc[:, a * HALF_S : (a + 1) * HALF_S], r, a, stationary1, moving)
+            send(acc[:], r, 0, S)
+
+        for r, tag in enumerate(("d_k1", "d_k2", None, None)):
+            finish(r, tag)

@@ -21,6 +21,7 @@ PACK = 4
 HALF_S = S // 2
 HALF_H = H // 2
 WINDOW = 384
+SHARED_AT = {"z_bf0": 0, "x_offs1": 0, "picked1": 512}
 
 
 def entries(lst, first, count):
@@ -34,9 +35,12 @@ def tile_picked_cmixhisendtwo_none_p_kernel(
     with ExitStack() as ctx:
         lists = ctx.enter_context(tc.tile_pool(name="lists", bufs=1))
         sb = ctx.enter_context(tc.tile_pool(name="sb", bufs=1))
+        shared = ctx.enter_context(tc.tile_pool(name="shared", bufs=1))
         psum = ctx.enter_context(tc.psum_pool(name="psum", bufs=1))
 
         def tile(shape, dtype, name, tag=None):
+            if name in SHARED_AT:
+                return shared.tile(shape, dtype, name=name, align_bytes=64, offset=SHARED_AT[name])
             return sb.tile(shape, dtype, name=name, tag=tag or name, align_bytes=64)
 
         def load_list(src, name):
@@ -55,16 +59,16 @@ def tile_picked_cmixhisendtwo_none_p_kernel(
         nc.scalar.dma_start(d_bytes[0:P:8, :].bitcast(I32), d_scales[0].bitcast(I32))
         k1_l = load_list(k1, "k1_l")
         k2_l = load_list(k2, "k2_l")
-        w_raw = tile([P, PACK, H], F32, "w_raw")
-        nc.sync.dma_start(w_raw[:], w1.rearrange("(p j) c -> p j c", j=PACK))
         gains = tile([P, PACK], F32, "gains")
         nc.sync.dma_start(gains[:], gs.rearrange("(p t) o -> p (t o)", t=PACK))
-        n1_l = load_list(n1, "n1_l")
-        n2_l = load_list(n2, "n2_l")
-        x_table = tile([P, T], I32, "x_table")
-        nc.sync.dma_start(x_table[:], x_words[0].rearrange("p c r -> p (c r)").bitcast(I32))
+        w_raw = tile([P, PACK, H], F32, "w_raw")
+        nc.sync.dma_start(w_raw[:], w1.rearrange("(p j) c -> p j c", j=PACK))
         d_table = tile([P, G], I32, "d_table")
         nc.sync.dma_start(d_table[:], d_words[0].rearrange("p c r -> p (c r)").bitcast(I32))
+        x_table = tile([P, T], I32, "x_table")
+        nc.sync.dma_start(x_table[:], x_words[0].rearrange("p c r -> p (c r)").bitcast(I32))
+        n1_l = load_list(n1, "n1_l")
+        n2_l = load_list(n2, "n2_l")
 
         def pick_scales(name, tag, picks):
             picked = tile([P, sum(pick[3] for pick in picks)], U8, name, tag)
@@ -90,19 +94,15 @@ def tile_picked_cmixhisendtwo_none_p_kernel(
             [(x_bytes, offs_l, 0, S), (x_bytes, hz_l, 0, S), (d_bytes, k1_l, 0, HALF_H), (d_bytes, k2_l, 0, HALF_H)],
         )
 
-        w_bf = tile([P, PACK, P, PACK], BF16, "w_bf")
-        w_out = w_bf[:].rearrange("p t m j -> p m j t")
-        w_in = w_raw[:].rearrange("p j (m t) -> p m j t", t=PACK)
+        w_bf = tile([P, PACK, P, PACK], BF16, "w_bf", "d_words")
+        plane0 = move_scales("plane0", None, nc.sync, picked0)
+        w_out = w_bf[:].rearrange("p t m j -> p m t j")
+        w_in = w_raw[:].rearrange("p j (m t) -> p m t j", t=PACK)
         nc.scalar.activation(w_out[:, 48:], w_in[:, 48:], COPY)
         nc.vector.tensor_copy(w_out[:, :48], w_in[:, :48])
-        plane0 = move_scales("plane0", "w_raw", nc.scalar, picked0)
         offs_scales, hz_scales = plane0[:, :S], plane0[:, S : 2 * S]
         k1_scales0, k2_scales0 = plane0[:, 2 * S : 2 * S + HALF_H], plane0[:, 2 * S + HALF_H :]
 
-        x_offs0 = tile([P, HALF_S], U32, "x_offs0")
-        x_hz0 = tile([P, HALF_S], U32, "x_hz0")
-        gather_words(x_offs0[:], x_table, offs_l, 0, HALF_S)
-        gather_words(x_hz0[:], x_table, hz_l, 0, HALF_S)
         w_codes = tile([P, H], U32, "w_codes")
         w_scales = tile([P, H], U8, "w_scales")
         nc.vector.quantize_mx(
@@ -137,10 +137,10 @@ def tile_picked_cmixhisendtwo_none_p_kernel(
             return z_codes[:], z_scales[:]
 
         def gather_d(c):
-            d_k2 = tile([P, HALF_H], U32, f"d_k2_{c}", "d_k2")
-            d_k1 = tile([P, HALF_H], U32, f"d_k1_{c}", "d_k1")
-            gather_words(d_k2[:], d_table, k2_l, c * HALF_H, HALF_H)
-            gather_words(d_k1[:], d_table, k1_l, c * HALF_H, HALF_H)
+            picked_d = tile([P, 2 * HALF_H], U32, f"picked_d{c}", "d_words")
+            d_k2, d_k1 = picked_d[:, :HALF_H], picked_d[:, HALF_H:]
+            gather_words(d_k2, d_table, k2_l, c * HALF_H, HALF_H)
+            gather_words(d_k1, d_table, k1_l, c * HALF_H, HALF_H)
             return d_k1, d_k2
 
         def make_h(acc, r, a, stationary, moving):
@@ -182,23 +182,26 @@ def tile_picked_cmixhisendtwo_none_p_kernel(
             nc.vector.tensor_tensor(best[:], windows[r][0][:, :S], windows[r][1][:, :S], MAX)
             nc.sync.dma_start(out[r * P : (r + 1) * P, :], best[:])
 
-        moving0 = (*make_z(0, x_offs0[:]), x_hz0[:])
         stationary0 = (*gather_d(0), k1_scales0, k2_scales0)
+        x_offs0 = tile([P, HALF_S], U32, "x_offs0")
+        gather_words(x_offs0[:], x_table, offs_l, 0, HALF_S)
+        x_hz = tile([P, S], U32, "x_hz")
+        gather_words(x_hz[:], x_table, hz_l, 0, S)
+        moving0 = (*make_z(0, x_offs0[:]), x_hz[:, :HALF_S])
         for r in range(2):
             acc = psum.tile([P, HALF_S], F32, name=f"h{r}_0")
             make_h(acc[:], r, 0, stationary0, moving0)
             send(acc[:], r, 0, HALF_S)
 
-        x_both1 = tile([P, S], U32, "x_both1", "z_bf0")
-        gather_words(x_both1[:, :HALF_S], x_table, offs_l, HALF_S, HALF_S)
-        gather_words(x_both1[:, HALF_S:], x_table, hz_l, HALF_S, HALF_S)
-        moving1 = (*make_z(1, x_both1[:, :HALF_S]), x_both1[:, HALF_S:])
+        x_offs1 = tile([P, HALF_S], U32, "x_offs1", "z_bf0")
+        gather_words(x_offs1[:], x_table, offs_l, HALF_S, HALF_S)
+        moving1 = (*make_z(1, x_offs1[:]), x_hz[:, HALF_S:])
         for r in range(2):
             acc = psum.tile([P, HALF_S], F32, name=f"h{r}_1")
             make_h(acc[:], r, 1, stationary0, moving1)
             send(acc[:], r, HALF_S, HALF_S)
 
-        picked1 = pick_scales("picked1", "z_bf1", [(d_bytes, k1_l, HALF_H, HALF_H), (d_bytes, k2_l, HALF_H, HALF_H)])
+        picked1 = pick_scales("picked1", "z_bf0", [(d_bytes, k1_l, HALF_H, HALF_H), (d_bytes, k2_l, HALF_H, HALF_H)])
         plane1 = move_scales("plane1", None, nc.sync, picked1)
         k1_scales1, k2_scales1 = plane1[:, :HALF_H], plane1[:, HALF_H:]
         stationary1 = (*gather_d(1), k1_scales1, k2_scales1)
@@ -208,5 +211,5 @@ def tile_picked_cmixhisendtwo_none_p_kernel(
                 make_h(acc[:, a * HALF_S : (a + 1) * HALF_S], r, a, stationary1, moving)
             send(acc[:], r, 0, S)
 
-        for r, tag in enumerate(("d_k1", "d_k2", None, None)):
+        for r, tag in enumerate(("d_words", "x_hz", None, None)):
             finish(r, tag)

@@ -54,19 +54,19 @@ def tile_picked_cmixhisendtwo_none_p_kernel(
         nc.gpsimd.memset(d_bytes[:].bitcast(I32), 0)
 
         offs_l = load_list(offs, "offs_l")
-        hz_l = load_list(hz, "hz_l")
-        nc.scalar.dma_start(x_bytes[0:P:8, :].bitcast(I32), x_scales[0].bitcast(I32))
-        nc.scalar.dma_start(d_bytes[0:P:8, :].bitcast(I32), d_scales[0].bitcast(I32))
-        k1_l = load_list(k1, "k1_l")
-        k2_l = load_list(k2, "k2_l")
         gains = tile([P, PACK], F32, "gains")
-        nc.sync.dma_start(gains[:], gs.rearrange("(p t) o -> p (t o)", t=PACK))
+        nc.scalar.dma_start(gains[:], gs.rearrange("(p t) o -> p (t o)", t=PACK))
+        hz_l = load_list(hz, "hz_l")
         w_raw = tile([P, PACK, H], F32, "w_raw")
-        nc.sync.dma_start(w_raw[:], w1.rearrange("(p j) c -> p j c", j=PACK))
+        nc.scalar.dma_start(w_raw[:], w1.rearrange("(p j) c -> p j c", j=PACK))
+        nc.sync.dma_start(x_bytes[0:P:8, :].bitcast(I32), x_scales[0].bitcast(I32))
+        nc.sync.dma_start(d_bytes[0:P:8, :].bitcast(I32), d_scales[0].bitcast(I32))
+        k1_l = load_list(k1, "k1_l")
+        x_table = tile([P, T], I32, "x_table")
+        nc.scalar.dma_start(x_table[:], x_words[0].rearrange("p c r -> p (c r)").bitcast(I32))
+        k2_l = load_list(k2, "k2_l")
         d_table = tile([P, G], I32, "d_table")
         nc.sync.dma_start(d_table[:], d_words[0].rearrange("p c r -> p (c r)").bitcast(I32))
-        x_table = tile([P, T], I32, "x_table")
-        nc.sync.dma_start(x_table[:], x_words[0].rearrange("p c r -> p (c r)").bitcast(I32))
         n1_l = load_list(n1, "n1_l")
         n2_l = load_list(n2, "n2_l")
 
@@ -182,12 +182,12 @@ def tile_picked_cmixhisendtwo_none_p_kernel(
             nc.vector.tensor_tensor(best[:], windows[r][0][:, :S], windows[r][1][:, :S], MAX)
             nc.sync.dma_start(out[r * P : (r + 1) * P, :], best[:])
 
-        stationary0 = (*gather_d(0), k1_scales0, k2_scales0)
         x_offs0 = tile([P, HALF_S], U32, "x_offs0")
         gather_words(x_offs0[:], x_table, offs_l, 0, HALF_S)
-        x_hz = tile([P, S], U32, "x_hz")
-        gather_words(x_hz[:], x_table, hz_l, 0, S)
-        moving0 = (*make_z(0, x_offs0[:]), x_hz[:, :HALF_S])
+        x_hz0 = tile([P, HALF_S], U32, "x_hz0")
+        gather_words(x_hz0[:], x_table, hz_l, 0, HALF_S)
+        moving0 = (*make_z(0, x_offs0[:]), x_hz0[:])
+        stationary0 = (*gather_d(0), k1_scales0, k2_scales0)
         for r in range(2):
             acc = psum.tile([P, HALF_S], F32, name=f"h{r}_0")
             make_h(acc[:], r, 0, stationary0, moving0)
@@ -195,7 +195,10 @@ def tile_picked_cmixhisendtwo_none_p_kernel(
 
         x_offs1 = tile([P, HALF_S], U32, "x_offs1", "z_bf0")
         gather_words(x_offs1[:], x_table, offs_l, HALF_S, HALF_S)
-        moving1 = (*make_z(1, x_offs1[:]), x_hz[:, HALF_S:])
+        z1 = make_z(1, x_offs1[:])
+        x_hz1 = tile([P, HALF_S], U32, "x_hz1", "w_codes")
+        gather_words(x_hz1[:], x_table, hz_l, HALF_S, HALF_S)
+        moving1 = (*z1, x_hz1[:])
         for r in range(2):
             acc = psum.tile([P, HALF_S], F32, name=f"h{r}_1")
             make_h(acc[:], r, 1, stationary0, moving1)
@@ -211,5 +214,5 @@ def tile_picked_cmixhisendtwo_none_p_kernel(
                 make_h(acc[:, a * HALF_S : (a + 1) * HALF_S], r, a, stationary1, moving)
             send(acc[:], r, 0, S)
 
-        for r, tag in enumerate(("d_words", "x_hz", None, None)):
+        for r, tag in enumerate(("d_words", "x_hz0", None, None)):
             finish(r, tag)

@@ -96,8 +96,8 @@ def tile_picked_cmixhisendtwo_none_p_kernel(
 
         w_bf = tile([P, PACK, P, PACK], BF16, "w_bf", "d_words")
         plane0 = move_scales("plane0", None, nc.sync, picked0)
-        w_out = w_bf[:].rearrange("p t m j -> p m t j")
-        w_in = w_raw[:].rearrange("p j (m t) -> p m t j", t=PACK)
+        w_out = w_bf[:].rearrange("p t m j -> p m j t")
+        w_in = w_raw[:].rearrange("p j (m t) -> p m j t", t=PACK)
         nc.scalar.activation(w_out[:, 48:], w_in[:, 48:], COPY)
         nc.vector.tensor_copy(w_out[:, :48], w_in[:, :48])
         offs_scales, hz_scales = plane0[:, :S], plane0[:, S : 2 * S]

from contextlib import ExitStack

import concourse.mybir as mybir

K, T, S, H, G = 512, 1024, 256, 512, 2048
FLOPS = 3 * 2 * K * H * S

F32 = mybir.dt.float32
BF16 = mybir.dt.bfloat16
I32 = mybir.dt.int32
U32 = mybir.dt.uint32
U16 = mybir.dt.uint16
U8 = mybir.dt.uint8
FP8X4 = mybir.dt.float8_e4m3fn_x4
COPY = mybir.ActivationFunctionType.Copy
MULT = mybir.AluOpType.mult
MAX = mybir.AluOpType.max

P = 128
PACK = 4
HALF_S = S // 2
HALF_H = H // 2
WINDOW = 384
SHARED_AT = {"z_bf0": 0, "x_offs1": 0, "picked1": 512}


def entries(lst, first, count):
    return lst[:, first // 16 : (first + count) // 16]


def tile_picked_cmixhisendtwo_none_p_kernel(
    tc, x_words, x_scales, w1, gs, d_words, d_scales, offs, k1, k2, hz, n1, n2, out
):
    nc = tc.nc
    with ExitStack() as ctx:
        lists = ctx.enter_context(tc.tile_pool(name="lists", bufs=1))
        sb = ctx.enter_context(tc.tile_pool(name="sb", bufs=1))
        shared = ctx.enter_context(tc.tile_pool(name="shared", bufs=1))
        psum = ctx.enter_context(tc.psum_pool(name="psum", bufs=1))

        def tile(shape, dtype, name, tag=None):
            if name in SHARED_AT:
                return shared.tile(shape, dtype, name=name, align_bytes=64, offset=SHARED_AT[name])
            return sb.tile(shape, dtype, name=name, tag=tag or name, align_bytes=64)

        def load_list(src, name):
            lst = lists.tile([P, src.shape[1]], U16, name=name)
            nc.sync.dma_start(lst[:], src)
            return lst

        x_bytes = tile([P, T], U8, "x_bytes")
        d_bytes = tile([P, G], U8, "d_bytes")
        nc.vector.memset(x_bytes[:].bitcast(I32), 0)
        nc.gpsimd.memset(d_bytes[:].bitcast(I32), 0)

        offs_l = load_list(offs, "offs_l")
        gains = tile([P, PACK], F32, "gains")
        nc.scalar.dma_start(gains[:], gs.rearrange("(p t) o -> p (t o)", t=PACK))
        hz_l = load_list(hz, "hz_l")
        w_raw = tile([P, PACK, H], F32, "w_raw")
        nc.scalar.dma_start(w_raw[:], w1.rearrange("(p j) c -> p j c", j=PACK))
        nc.sync.dma_start(x_bytes[0:P:8, :].bitcast(I32), x_scales[0].bitcast(I32))
        nc.sync.dma_start(d_bytes[0:P:8, :].bitcast(I32), d_scales[0].bitcast(I32))
        k1_l = load_list(k1, "k1_l")
        x_table = tile([P, T], I32, "x_table")
        nc.scalar.dma_start(x_table[:], x_words[0].rearrange("p c r -> p (c r)").bitcast(I32))
        k2_l = load_list(k2, "k2_l")
        d_table = tile([P, G], I32, "d_table")
        nc.sync.dma_start(d_table[:], d_words[0].rearrange("p c r -> p (c r)").bitcast(I32))
        n1_l = load_list(n1, "n1_l")
        n2_l = load_list(n2, "n2_l")

        def pick_scales(name, tag, picks):
            picked = tile([P, sum(pick[3] for pick in picks)], U8, name, tag)
            at = 0
            for table, lst, first, count in picks:
                nc.vector.tensor_copy(picked[:, at : at + count], table[:].indirect(entries(lst, first, count)))
                at = at + count
            return picked

        def move_scales(name, tag, queue, picked):
            plane = tile(picked.shape, U8, name, tag)
            nc.vector.memset(plane[:].bitcast(I32), 0)
            for b in range(4):
                queue.dma_start(plane[b:P:32, :].bitcast(I32), picked[8 * b : P : 32, :].bitcast(I32))
            return plane

        def gather_words(words, table, lst, first, count):
            nc.vector.tensor_copy(words, table[:].bitcast(U32).indirect(entries(lst, first, count)))

        picked0 = pick_scales(
            "picked0",
            None,
            [(x_bytes, offs_l, 0, S), (x_bytes, hz_l, 0, S), (d_bytes, k1_l, 0, HALF_H), (d_bytes, k2_l, 0, HALF_H)],
        )

        w_bf = tile([P, PACK, P, PACK], BF16, "w_bf", "d_words")
        plane0 = move_scales("plane0", None, nc.sync, picked0)
        w_out = w_bf[:].rearrange("p t m j -> p m j t")
        w_in = w_raw[:].rearrange("p j (m t) -> p m j t", t=PACK)
        nc.scalar.activation(w_out[:, 48:], w_in[:, 48:], COPY)
        nc.vector.tensor_copy(w_out[:, :48], w_in[:, :48])
        offs_scales, hz_scales = plane0[:, :S], plane0[:, S : 2 * S]
        k1_scales0, k2_scales0 = plane0[:, 2 * S : 2 * S + HALF_H], plane0[:, 2 * S + HALF_H :]

        w_codes = tile([P, H], U32, "w_codes")
        w_scales = tile([P, H], U8, "w_scales")
        nc.vector.quantize_mx(
            out=w_codes[:].bitcast(FP8X4), scales=w_scales[:], in_=w_bf[:].rearrange("p t m j -> p (t m j)")
        )

        def make_z(a, x_offs):
            y = psum.tile([P, PACK, HALF_S], F32, name=f"y{a}")
            for t in range(PACK):
                cols = slice(t * P, (t + 1) * P)
                nc.tensor.matmul_mx(
                    out=y[:, t, :],
                    lhsT=w_codes[:, cols].bitcast(FP8X4),
                    lhsT_scale=w_scales[:, cols],
                    rhs=x_offs.bitcast(FP8X4),
                    rhs_scale=offs_scales[:, a * HALF_S : (a + 1) * HALF_S],
                    start=True,
                    stop=True,
                )
            z_bf = tile([P, HALF_S, PACK], BF16, f"z_bf{a}")
            nc.vector.tensor_tensor(
                z_bf[:],
                y[:].rearrange("p t j -> p j t"),
                gains[:].unsqueeze(1).to_broadcast([P, HALF_S, PACK]),
                MULT,
            )
            z_codes = tile([P, HALF_S], U32, f"z_codes{a}")
            z_scales = tile([P, HALF_S], U8, f"z_scales{a}")
            nc.vector.quantize_mx(
                out=z_codes[:].bitcast(FP8X4), scales=z_scales[:], in_=z_bf[:].rearrange("p j t -> p (j t)")
            )
            return z_codes[:], z_scales[:]

        def gather_d(c):
            picked_d = tile([P, 2 * HALF_H], U32, f"picked_d{c}", "d_words")
            d_k2, d_k1 = picked_d[:, :HALF_H], picked_d[:, HALF_H:]
            gather_words(d_k2, d_table, k2_l, c * HALF_H, HALF_H)
            gather_words(d_k1, d_table, k1_l, c * HALF_H, HALF_H)
            return d_k1, d_k2

        def make_h(acc, r, a, stationary, moving):
            d_k1, d_k2, k1_scales, k2_scales = stationary
            z_codes, z_scales, x_hz = moving
            cols = slice(r % 2 * P, (r % 2 + 1) * P)
            nc.tensor.matmul_mx(
                out=acc,
                lhsT=d_k2[:, cols].bitcast(FP8X4),
                lhsT_scale=k2_scales[:, cols],
                rhs=x_hz.bitcast(FP8X4),
                rhs_scale=hz_scales[:, a * HALF_S : (a + 1) * HALF_S],
                start=True,
                stop=False,
            )
            nc.tensor.matmul_mx(
                out=acc,
                lhsT=d_k1[:, cols].bitcast(FP8X4),
                lhsT_scale=k1_scales[:, cols],
                rhs=z_codes.bitcast(FP8X4),
                rhs_scale=z_scales,
                start=False,
                stop=True,
            )

        windows = [[tile([P, WINDOW], F32, f"ds{u}_{r}") for u in range(2)] for r in range(H // P)]

        def send(acc, r, first, count):
            h = tile([P, count], F32, f"h{r}_{first}")
            if (r, first) == (0, 0):
                nc.scalar.activation(h[:], acc, COPY, scale=0.0625)
            else:
                nc.vector.tensor_scalar_mul(h[:], acc, 0.0625)
            for window, lst in zip(windows[r], (n1_l, n2_l)):
                nc.scalar.activation(window[:].indirect(entries(lst, first, count)), h[:], COPY)

        def finish(r, tag):
            best = tile([P, S], F32, f"best{r}", tag)
            nc.vector.tensor_tensor(best[:], windows[r][0][:, :S], windows[r][1][:, :S], MAX)
            nc.sync.dma_start(out[r * P : (r + 1) * P, :], best[:])

        x_offs0 = tile([P, HALF_S], U32, "x_offs0")
        gather_words(x_offs0[:], x_table, offs_l, 0, HALF_S)
        x_hz0 = tile([P, HALF_S], U32, "x_hz0")
        gather_words(x_hz0[:], x_table, hz_l, 0, HALF_S)
        moving0 = (*make_z(0, x_offs0[:]), x_hz0[:])
        stationary0 = (*gather_d(0), k1_scales0, k2_scales0)
        for r in range(2):
            acc = psum.tile([P, HALF_S], F32, name=f"h{r}_0")
            make_h(acc[:], r, 0, stationary0, moving0)
            send(acc[:], r, 0, HALF_S)

        x_offs1 = tile([P, HALF_S], U32, "x_offs1", "z_bf0")
        gather_words(x_offs1[:], x_table, offs_l, HALF_S, HALF_S)
        z1 = make_z(1, x_offs1[:])
        x_hz1 = tile([P, HALF_S], U32, "x_hz1", "w_codes")
        gather_words(x_hz1[:], x_table, hz_l, HALF_S, HALF_S)
        moving1 = (*z1, x_hz1[:])
        for r in range(2):
            acc = psum.tile([P, HALF_S], F32, name=f"h{r}_1")
            make_h(acc[:], r, 1, stationary0, moving1)
            send(acc[:], r, HALF_S, HALF_S)

        picked1 = pick_scales("picked1", "z_bf0", [(d_bytes, k1_l, HALF_H, HALF_H), (d_bytes, k2_l, HALF_H, HALF_H)])
        plane1 = move_scales("plane1", None, nc.sync, picked1)
        k1_scales1, k2_scales1 = plane1[:, :HALF_H], plane1[:, HALF_H:]
        stationary1 = (*gather_d(1), k1_scales1, k2_scales1)
        for r in range(2, 4):
            acc = psum.tile([P, S], F32, name=f"h{r}")
            for a, moving in enumerate((moving0, moving1)):
                make_h(acc[:, a * HALF_S : (a + 1) * HALF_S], r, a, stationary1, moving)
            send(acc[:], r, 0, S)

        for r, tag in enumerate(("d_words", "x_hz0", None, None)):
            finish(r, tag)
